import numpy as np
import ml_dtypes


def mxq(x, axis, fmt="e4m3"):
    dtype, down = {"e4m3": (ml_dtypes.float8_e4m3fn, 7), "e5m2": (ml_dtypes.float8_e5m2, 14)}[fmt]
    v = np.moveaxis(np.asarray(x, np.float32).astype(ml_dtypes.bfloat16).astype(np.float64), axis, -1)
    blocks = v.reshape(v.shape[:-1] + (-1, 32))
    amax = np.abs(blocks).max(-1, keepdims=True)
    byte = np.maximum(np.where(amax > 0, np.frexp(amax)[1] - 1 + 127, 0) - down, 1)
    scale = np.exp2(byte - 127.0)
    codes = (blocks / scale).astype(np.float32).astype(dtype).astype(np.float64)
    return np.moveaxis((codes * scale).reshape(v.shape), -1, axis)


WIDE = False


def mx_kscale(k):
    if not WIDE:
        return np.ones(k)
    levels = np.array([10, -10, 5, -5, 0])
    if k % 512:
        return np.exp2(np.random.permutation(np.resize(levels, k // 32))).repeat(32)
    a = np.empty((k // 512, 16))
    for p in range(k // 512):
        a[p, :8] = np.random.permutation(np.resize(levels, 8))
        for g in range(8):
            far = levels[np.abs(levels - a[p, g]) >= 10]
            a[p, g + 8] = far[np.random.randint(len(far))]
    return np.exp2(a.ravel()).repeat(32)


def f64(x):
    return np.asarray(x).astype(np.float64)


E2M1 = np.array([0.0, 0.5, 1.0, 1.5, 2.0, 3.0, 4.0, 6.0, -0.0, -0.5, -1.0, -1.5, -2.0, -3.0, -4.0, -6.0])


def pack_weight(w, fmt):
    k, n = w.shape
    w = f64(np.asarray(w, np.float32).astype(ml_dtypes.bfloat16)).reshape(k // 32, 32, n)
    amax = np.abs(w).max(1)
    if fmt == "e4m3":
        byte = np.frexp(amax)[1] - 1 + 127 - 7
    else:
        mant, ex = np.frexp(amax / 6.0)
        byte = np.where(mant > 0.5, ex, ex - 1) + 127
    byte = np.clip(np.where(amax > 0, byte, 1), 1, 254)
    scaled = (w * np.exp2(127.0 - byte)[:, None, :]).reshape(k, n).astype(np.float32)
    by_word = np.ascontiguousarray(scaled.reshape(k // 512, 128, 4, n).transpose(0, 1, 3, 2))
    if fmt == "e4m3":
        words = by_word.astype(ml_dtypes.float8_e4m3fn).view(np.uint8)
    else:
        c = by_word.astype(ml_dtypes.float4_e2m1fn).view(np.uint8) & 0xF
        words = (c[..., 0::2] | (c[..., 1::2] << 4)).reshape(k // 512, 128, 2 * n)
    return np.ascontiguousarray(words), np.ascontiguousarray(byte.astype(np.uint8).reshape(k // 512, 16, n))


def unpack_weight(words, scales, fmt):
    g, _, n = scales.shape
    words = np.ascontiguousarray(words).reshape(g, 128, n, -1)
    if fmt == "e4m3":
        vals = words.view(ml_dtypes.float8_e4m3fn).astype(np.float64)
    else:
        nib = np.empty((g, 128, n, 4), np.uint8)
        nib[..., 0::2] = words & 0xF
        nib[..., 1::2] = words >> 4
        vals = E2M1[nib]
    vals = vals * np.repeat(np.exp2(scales.astype(np.float64) - 127.0), 8, axis=1)[..., None]
    return vals.transpose(0, 1, 3, 2).reshape(g * 512, n)


def bf(x):
    return np.asarray(x, np.float32).astype(ml_dtypes.bfloat16)


def planes(Y):
    r, m = Y.shape
    b = f64(bf(Y)).reshape(r // 32, 32, m)
    amax = np.abs(b).max(1)
    byte = np.clip(np.where(amax > 0, np.frexp(amax)[1] - 1 + 127 - 7, 1), 1, 254)
    codes = (b * np.exp2(127.0 - byte)[:, None, :]).reshape(r, m).astype(np.float32).astype(ml_dtypes.float8_e4m3fn).view(np.uint8)
    words = codes.reshape(r // 512, 128, 4, m).transpose(0, 1, 3, 2)
    return np.ascontiguousarray(words), np.ascontiguousarray(byte.astype(np.uint8).reshape(r // 512, 16, m))


K, L, T, N = 1024, 512, 512, 512


def setup_inputs():
    n = np.random.standard_normal
    fk = mx_kscale(K)
    fl = mx_kscale(L)
    wap = pack_weight(n((K, N)) * 1 / np.sqrt(K) * fk[:, None], "e2m1")
    xsp = pack_weight(n((L, T)) / fl[:, None], "e4m3")
    wsp = pack_weight(n((L, N)) * 1 / np.sqrt(L) * fl[:, None], "e2m1")
    wcp = pack_weight(n((K, N)) * 1 / np.sqrt(K) * fk[:, None], "e4m3")
    return {
        "xt": (n((K, T)) * np.random.uniform(0.3, 1.7, (1, T)) / fk[:, None]).astype(np.float32),
        "wa_words": wap[0],
        "wa_scales": wap[1],
        "xs_words": xsp[0],
        "xs_scales": xsp[1],
        "ws_words": wsp[0],
        "ws_scales": wsp[1],
        "wc_words": wcp[0],
        "wc_scales": wcp[1],
    }


def reference(xt, wa_words, wa_scales, xs_words, xs_scales, ws_words, ws_scales, wc_words, wc_scales):
    wau = unpack_weight(wa_words, wa_scales, "e2m1")
    xsu = unpack_weight(xs_words, xs_scales, "e4m3")
    wsu = unpack_weight(ws_words, ws_scales, "e2m1")
    wcu = unpack_weight(wc_words, wc_scales, "e4m3")
    xtq = mxq(f64(xt), 0, "e4m3")
    a = xtq.T @ wau + xsu.T @ wsu
    b = xtq.T @ wcu
    sa = np.sqrt(np.mean(np.square(a), axis=1, keepdims=True) + 0.01)
    sb = np.sqrt(np.mean(np.square(b), axis=1, keepdims=True) + 0.01)
    y = a * sb / sa + 0.3 * b
    words, scales = planes(y)
    return y, words, scales

@@ -1,0 +1,204 @@
+import math
+from contextlib import ExitStack
+
+import concourse.mybir as mybir
+
+K, L, T, N = 1024, 512, 512, 512
+FLOPS = 2 * T * N * (K + L + K)
+
+F32 = mybir.dt.float32
+BF16 = mybir.dt.bfloat16
+I32 = mybir.dt.int32
+U8 = mybir.dt.uint8
+FP8X4 = mybir.dt.float8_e4m3fn_x4
+FP4X4 = mybir.dt.float4_e2m1fn_x4
+ACT = mybir.ActivationFunctionType
+ALU = mybir.AluOpType
+
+P = 128
+PACK = 4
+PASS = P * PACK
+EPS = 0.01
+RIVAL_SHARE = 0.3
+SQUARE_SCALE = 1.0 / math.sqrt(N * EPS)
+X_CAST_SPLIT = 84
+Y_CAST_SPLIT = 192
+HALF = N // 2
+
+
+def tile_mix_rows_sized_like_rival_pl_kernel(
+    tc, xt, wa_words, wa_scales, xs_words, xs_scales, ws_words, ws_scales, wc_words, wc_scales, out_0, out_1, out_2
+):
+    nc = tc.nc
+    with ExitStack() as ctx:
+        sb = ctx.enter_context(tc.tile_pool(name="sb", bufs=1))
+        ps = ctx.enter_context(tc.psum_pool(name="ps", bufs=1))
+        ctx.enter_context(tc.manual_schedule())
+
+        x_raw = [sb.tile([P, PACK, T], F32, name="x_raw%d" % g) for g in range(2)]
+        x_bf = [sb.tile([P, T * PACK], BF16, name="x_bf%d" % g, align_bytes=64) for g in range(2)]
+        x_codes = [sb.tile([P, T], I32, name="x_codes%d" % g, align_bytes=64) for g in range(2)]
+        x_plane = [sb.tile([P, T], U8, name="x_plane%d" % g, align_bytes=64) for g in range(2)]
+        wc_codes = [sb.tile([P, N], I32, name="wc_codes%d" % g, align_bytes=64) for g in range(2)]
+        wc_plane = sb.tile([P, 2, N], U8, align_bytes=64)
+        wa_codes = sb.tile([P, 2, 2 * N], U8, align_bytes=64)
+        wa_plane = sb.tile([P, 2, N], U8, align_bytes=64)
+        ws_codes = sb.tile([P, 2 * N], U8, align_bytes=64)
+        ws_plane = sb.tile([P, 1, N], U8, align_bytes=64)
+        xs_raw = sb.tile([P, T], I32, align_bytes=64)
+        xs_plane_raw = sb.tile([P, 1, T], U8, align_bytes=64)
+        xs_codes = sb.tile([P, T], I32, align_bytes=64)
+        xs_plane = sb.tile([P, T], U8, align_bytes=64)
+        b_part = [sb.tile([P, N], F32, name="b_part%d" % r) for r in range(PACK)]
+        y = sb.tile([P, PACK, N], F32)
+        y_bf = sb.tile([P, N * PACK], BF16, align_bytes=64)
+        y_codes = sb.tile([P, N], I32, align_bytes=64)
+        y_plane = sb.tile([P, N], U8, align_bytes=64)
+        sum_b = sb.tile([P, PACK], F32)
+        sum_b1 = sb.tile([P, PACK], F32)
+        inv_b = sb.tile([P, PACK], F32)
+        sum_a = sb.tile([P, PACK], F32)
+        gain = sb.tile([P, PACK], F32)
+        table = sb.tile([P, 1], F32)
+        acc_a = [ps.tile([P, N], F32, name="acc_a%d" % r) for r in range(PACK)]
+        acc_b = [ps.tile([P, N], F32, name="acc_b%d" % r) for r in range(PACK)]
+
+        def zero(engine, plane):
+            engine.memset(plane[:].rearrange("p g n -> p (g n)").bitcast(I32), 0)
+
+        def load_plane(queue, plane, scales):
+            for r in range(4):
+                queue.dma_start(
+                    out=plane[:].bitcast(I32)[r:P:32],
+                    in_=scales.bitcast(I32)[:, r:16:4, :].rearrange("g q n -> q g n"),
+                )
+
+        def load_x(g):
+            nc.sync.dma_start(out=x_raw[g][:], in_=xt[g * PASS : (g + 1) * PASS, :].rearrange("(p j) t -> p j t", j=PACK))
+
+        def load_words(tile, words):
+            nc.sync.dma_start(out=tile[:], in_=words.rearrange("p n t -> p (n t)").bitcast(I32))
+
+        def cast_x(g):
+            src = x_raw[g][:].rearrange("p j (m r) -> p m j r", r=PACK)
+            dst = x_bf[g][:].rearrange("p (r m j) -> p m j r", r=PACK, j=PACK)
+            nc.vector.tensor_copy(out=dst[:, :X_CAST_SPLIT], in_=src[:, :X_CAST_SPLIT])
+            nc.scalar.copy(out=dst[:, X_CAST_SPLIT:], in_=src[:, X_CAST_SPLIT:])
+
+        def quantize(codes, plane, values, first, count):
+            nc.vector.quantize_mx(
+                out=codes[:, first : first + count].bitcast(FP8X4),
+                scales=plane[:, first : first + count],
+                in_=values[:, PACK * first : PACK * (first + count)],
+            )
+
+        def product(acc, codes, plane, r, w, w_plane, start, stop):
+            cols = slice(r * P, (r + 1) * P)
+            nc.tensor.matmul_mx(
+                out=acc[:], lhsT=codes[:, cols].bitcast(FP8X4), lhsT_scale=plane[:, cols],
+                rhs=w, rhs_scale=w_plane, start=start, stop=stop,
+            )
+
+        def sum_squares(acc, sums, r):
+            nc.scalar.activation(
+                out=y[:, r, :], in_=acc[r][:], func=ACT.Square, scale=SQUARE_SCALE, accum_out=sums[:, r : r + 1]
+            )
+
+        def row_gain(r):
+            col = slice(r, r + 1)
+            nc.scalar.activation(
+                out=gain[:, col], in_=sum_a[:, col], func=ACT.Abs_reciprocal_sqrt, scale=inv_b[:, col], bias=inv_b[:, col]
+            )
+
+        def take_b(r):
+            nc.vector.tensor_scalar(out=b_part[r][:], in0=acc_b[r][:], scalar1=RIVAL_SHARE, scalar2=None, op0=ALU.mult)
+
+        def add_one(cols):
+            nc.vector.tensor_scalar(out=sum_b1[:, cols], in0=sum_b[:, cols], scalar1=1.0, scalar2=None, op0=ALU.add)
+
+        def invert(cols):
+            nc.vector.reciprocal(out=inv_b[:, cols], in_=sum_b1[:, cols])
+
+        out_rows = out_0.rearrange("(p r) n -> p r n", r=PACK)
+
+        def combine(r, cols):
+            nc.vector.scalar_tensor_tensor(
+                out=y[:, r, cols], in0=acc_a[r][:, cols], scalar=gain[:, r : r + 1], in1=b_part[r][:, cols],
+                op0=ALU.mult, op1=ALU.add,
+            )
+            nc.sync.dma_start(out=out_rows[:, r, cols], in_=y[:, r, cols])
+
+        zero(nc.vector, wc_plane)
+        zero(nc.vector, wa_plane)
+        zero(nc.vector, ws_plane)
+        nc.vector.memset(table[:], 1.0)
+        nc.scalar.activation(out=gain[:, 0:1], in_=table[:], func=ACT.Abs_reciprocal_sqrt)
+        zero(nc.gpsimd, xs_plane_raw)
+        load_plane(nc.gpsimd, xs_plane_raw, xs_scales)
+        load_x(0)
+        load_plane(nc.sync, wc_plane, wc_scales)
+        load_words(wc_codes[0], wc_words[0])
+        load_x(1)
+        load_words(wc_codes[1], wc_words[1])
+        load_plane(nc.sync, wa_plane, wa_scales)
+        nc.sync.dma_start(out=wa_codes[:].bitcast(I32), in_=wa_words.bitcast(I32).rearrange("g p n -> p g n"))
+        load_words(xs_raw, xs_words[0])
+        nc.sync.dma_start(out=ws_codes[:].bitcast(I32), in_=ws_words[0].bitcast(I32))
+        load_plane(nc.sync, ws_plane, ws_scales)
+
+        cast_x(0)
+        quantize(x_codes[0], x_plane[0], x_bf[0], 0, T)
+        for r in range(PACK):
+            product(acc_b[r], x_codes[0], x_plane[0], r, wc_codes[0][:].bitcast(FP8X4), wc_plane[:, 0, :], True, False)
+        nc.vector.tensor_copy(
+            out=xs_plane[:].rearrange("p (r m) -> p m r", r=PACK),
+            in_=xs_plane_raw[:, 0, :].rearrange("p (m r) -> p m r", r=PACK),
+        )
+
+        cast_x(1)
+        for r in range(PACK):
+            quantize(x_codes[1], x_plane[1], x_bf[1], r * P, P)
+            product(acc_b[r], x_codes[1], x_plane[1], r, wc_codes[1][:].bitcast(FP8X4), wc_plane[:, 1, :], False, True)
+        for r in range(PACK):
+            nc.gpsimd.tensor_copy(out=xs_codes[:, r * P : (r + 1) * P], in_=xs_raw[:, r:T:PACK])
+        for r in range(PACK):
+            for g in range(2):
+                product(acc_a[r], x_codes[g], x_plane[g], r, wa_codes[:, g, :].bitcast(FP4X4), wa_plane[:, g, :], g == 0, False)
+            product(acc_a[r], xs_codes, xs_plane, r, ws_codes[:].bitcast(FP4X4), ws_plane[:, 0, :], False, True)
+
+        last = PACK - 1
+        for r in range(last):
+            sum_squares(acc_b, sum_b, r)
+            take_b(r)
+        add_one(slice(0, last))
+        invert(slice(0, last))
+        sum_squares(acc_a, sum_a, 0)
+        sum_squares(acc_b, sum_b, last)
+        row_gain(0)
+        combine(0, slice(0, N))
+        add_one(slice(last, PACK))
+        take_b(last)
+        invert(slice(last, PACK))
+        for r in range(1, PACK):
+            sum_squares(acc_a, sum_a, r)
+            row_gain(r)
+            if r < last:
+                combine(r, slice(0, N))
+
+        src = y[:].rearrange("p r (c i) -> p c r i", i=4)
+        dst = y_bf[:].rearrange("p (c i r) -> p c r i", i=4, r=PACK)
+        split = Y_CAST_SPLIT // 4
+        half = HALF // 4
+        words_out = out_1[0].rearrange("p n t -> p (n t)").bitcast(I32)
+        combine(last, slice(0, HALF))
+        nc.scalar.copy(out=dst[:, :split], in_=src[:, :split])
+        combine(last, slice(HALF, N))
+        nc.vector.tensor_copy(out=dst[:, half:], in_=src[:, half:])
+        nc.vector.tensor_copy(out=dst[:, split:half], in_=src[:, split:half])
+        quantize(y_codes, y_plane, y_bf, HALF, HALF)
+        nc.sync.dma_start(out=words_out[:, HALF:], in_=y_codes[:, HALF:])
+        quantize(y_codes, y_plane, y_bf, 0, HALF)
+        nc.sync.dma_start(out=words_out[:, :HALF], in_=y_codes[:, :HALF])
+        for q in range(4):
+            queue = nc.scalar if q % 2 == 0 else nc.sync
+            queue.dma_start(out=out_2[0].bitcast(I32)[4 * q : 4 * q + 4, :], in_=y_plane[:].bitcast(I32)[32 * q : 32 * q + 4, :])

@@ -21,9 +21,9 @@ PASS = P * PACK
 EPS = 0.01
 RIVAL_SHARE = 0.3
 SQUARE_SCALE = 1.0 / math.sqrt(N * EPS)
-X_CAST_SPLIT = 84
-Y_CAST_SPLIT = 192
 HALF = N // 2
+X_LOADS = ((0, 0, 4), (1, 0, 2), (1, 2, 2))
+Y_CAST_SPLIT = 208
 
 
 def tile_mix_rows_sized_like_rival_pl_kernel(
@@ -35,7 +35,7 @@ def tile_mix_rows_sized_like_rival_pl_kernel(
         ps = ctx.enter_context(tc.psum_pool(name="ps", bufs=1))
         ctx.enter_context(tc.manual_schedule())
 
-        x_raw = [sb.tile([P, PACK, T], F32, name="x_raw%d" % g) for g in range(2)]
+        x_raw = [sb.tile([P, count, T], F32, name="x_raw%d" % i) for i, (g, first, count) in enumerate(X_LOADS)]
         x_bf = [sb.tile([P, T * PACK], BF16, name="x_bf%d" % g, align_bytes=64) for g in range(2)]
         x_codes = [sb.tile([P, T], I32, name="x_codes%d" % g, align_bytes=64) for g in range(2)]
         x_plane = [sb.tile([P, T], U8, name="x_plane%d" % g, align_bytes=64) for g in range(2)]
@@ -73,17 +73,20 @@ def tile_mix_rows_sized_like_rival_pl_kernel(
                     in_=scales.bitcast(I32)[:, r:16:4, :].rearrange("g q n -> q g n"),
                 )
 
-        def load_x(g):
-            nc.sync.dma_start(out=x_raw[g][:], in_=xt[g * PASS : (g + 1) * PASS, :].rearrange("(p j) t -> p j t", j=PACK))
+        def load_x(i):
+            g, first, count = X_LOADS[i]
+            rows = xt[g * PASS : (g + 1) * PASS, :].rearrange("(p j) t -> p j t", j=PACK)
+            nc.sync.dma_start(out=x_raw[i][:], in_=rows[:, first : first + count, :])
 
         def load_words(tile, words):
             nc.sync.dma_start(out=tile[:], in_=words.rearrange("p n t -> p (n t)").bitcast(I32))
 
-        def cast_x(g):
-            src = x_raw[g][:].rearrange("p j (m r) -> p m j r", r=PACK)
-            dst = x_bf[g][:].rearrange("p (r m j) -> p m j r", r=PACK, j=PACK)
-            nc.vector.tensor_copy(out=dst[:, :X_CAST_SPLIT], in_=src[:, :X_CAST_SPLIT])
-            nc.scalar.copy(out=dst[:, X_CAST_SPLIT:], in_=src[:, X_CAST_SPLIT:])
+        def cast_x(i):
+            g, first, count = X_LOADS[i]
+            src = x_raw[i][:].rearrange("p j (m r) -> p m j r", r=PACK)
+            dst = x_bf[g][:].rearrange("p (r m j) -> p m j r", r=PACK, j=PACK)[:, :, first : first + count, :]
+            nc.vector.tensor_copy(out=dst[:, :, :, :2], in_=src[:, :, :, :2])
+            nc.scalar.copy(out=dst[:, :, :, 2:], in_=src[:, :, :, 2:])
 
         def quantize(codes, plane, values, first, count):
             nc.vector.quantize_mx(
@@ -113,6 +116,12 @@ def tile_mix_rows_sized_like_rival_pl_kernel(
         def take_b(r):
             nc.vector.tensor_scalar(out=b_part[r][:], in0=acc_b[r][:], scalar1=RIVAL_SHARE, scalar2=None, op0=ALU.mult)
 
+        def sum_squares_on_vector(r):
+            nc.vector.scalar_tensor_tensor(
+                out=y[:, r, :], in0=acc_b[r][:], scalar=1.0 / (RIVAL_SHARE * N * EPS), in1=b_part[r][:],
+                op0=ALU.mult, op1=ALU.mult, accum_out=sum_b[:, r : r + 1],
+            )
+
         def add_one(cols):
             nc.vector.tensor_scalar(out=sum_b1[:, cols], in0=sum_b[:, cols], scalar1=1.0, scalar2=None, op0=ALU.add)
 
@@ -126,7 +135,9 @@ def tile_mix_rows_sized_like_rival_pl_kernel(
                 out=y[:, r, cols], in0=acc_a[r][:, cols], scalar=gain[:, r : r + 1], in1=b_part[r][:, cols],
                 op0=ALU.mult, op1=ALU.add,
             )
-            nc.sync.dma_start(out=out_rows[:, r, cols], in_=y[:, r, cols])
+
+        def store_rows(rows, cols):
+            nc.sync.dma_start(out=out_rows[:, rows, cols], in_=y[:, rows, cols])
 
         zero(nc.vector, wc_plane)
         zero(nc.vector, wa_plane)
@@ -139,62 +150,68 @@ def tile_mix_rows_sized_like_rival_pl_kernel(
         load_plane(nc.sync, wc_plane, wc_scales)
         load_words(wc_codes[0], wc_words[0])
         load_x(1)
-        load_words(wc_codes[1], wc_words[1])
+        load_x(2)
         load_plane(nc.sync, wa_plane, wa_scales)
+        load_words(wc_codes[1], wc_words[1])
         nc.sync.dma_start(out=wa_codes[:].bitcast(I32), in_=wa_words.bitcast(I32).rearrange("g p n -> p g n"))
         load_words(xs_raw, xs_words[0])
         nc.sync.dma_start(out=ws_codes[:].bitcast(I32), in_=ws_words[0].bitcast(I32))
         load_plane(nc.sync, ws_plane, ws_scales)
 
         cast_x(0)
-        quantize(x_codes[0], x_plane[0], x_bf[0], 0, T)
         for r in range(PACK):
+            quantize(x_codes[0], x_plane[0], x_bf[0], r * P, P)
             product(acc_b[r], x_codes[0], x_plane[0], r, wc_codes[0][:].bitcast(FP8X4), wc_plane[:, 0, :], True, False)
-        nc.vector.tensor_copy(
-            out=xs_plane[:].rearrange("p (r m) -> p m r", r=PACK),
-            in_=xs_plane_raw[:, 0, :].rearrange("p (m r) -> p m r", r=PACK),
-        )
 
         cast_x(1)
+        cast_x(2)
         for r in range(PACK):
             quantize(x_codes[1], x_plane[1], x_bf[1], r * P, P)
             product(acc_b[r], x_codes[1], x_plane[1], r, wc_codes[1][:].bitcast(FP8X4), wc_plane[:, 1, :], False, True)
         for r in range(PACK):
             nc.gpsimd.tensor_copy(out=xs_codes[:, r * P : (r + 1) * P], in_=xs_raw[:, r:T:PACK])
+            nc.gpsimd.tensor_copy(out=xs_plane[:, r * P : (r + 1) * P], in_=xs_plane_raw[:, 0, r:T:PACK])
         for r in range(PACK):
             for g in range(2):
                 product(acc_a[r], x_codes[g], x_plane[g], r, wa_codes[:, g, :].bitcast(FP4X4), wa_plane[:, g, :], g == 0, False)
             product(acc_a[r], xs_codes, xs_plane, r, ws_codes[:].bitcast(FP4X4), ws_plane[:, 0, :], False, True)
 
         last = PACK - 1
-        for r in range(last):
-            sum_squares(acc_b, sum_b, r)
-            take_b(r)
-        add_one(slice(0, last))
-        invert(slice(0, last))
-        sum_squares(acc_a, sum_a, 0)
-        sum_squares(acc_b, sum_b, last)
-        row_gain(0)
-        combine(0, slice(0, N))
-        add_one(slice(last, PACK))
+        whole = slice(0, N)
+        take_b(0)
+        sum_squares(acc_b, sum_b, 1)
+        take_b(2)
+        sum_squares(acc_b, sum_b, 0)
+        take_b(1)
+        sum_squares(acc_b, sum_b, 2)
         take_b(last)
+        add_one(slice(0, last))
+        sum_squares_on_vector(last)
+        invert(slice(0, last))
+        add_one(slice(last, PACK))
+        sum_squares(acc_a, sum_a, 0)
+        sum_squares(acc_a, sum_a, 1)
+        row_gain(0)
+        combine(0, whole)
+        store_rows(slice(0, 1), whole)
         invert(slice(last, PACK))
         for r in range(1, PACK):
-            sum_squares(acc_a, sum_a, r)
+            if r > 1:
+                sum_squares(acc_a, sum_a, r)
             row_gain(r)
             if r < last:
-                combine(r, slice(0, N))
+                combine(r, whole)
+                store_rows(slice(r, r + 1), whole)
 
         src = y[:].rearrange("p r (c i) -> p c r i", i=4)
         dst = y_bf[:].rearrange("p (c i r) -> p c r i", i=4, r=PACK)
-        split = Y_CAST_SPLIT // 4
-        half = HALF // 4
         words_out = out_1[0].rearrange("p n t -> p (n t)").bitcast(I32)
         combine(last, slice(0, HALF))
-        nc.scalar.copy(out=dst[:, :split], in_=src[:, :split])
+        nc.scalar.copy(out=dst[:, : Y_CAST_SPLIT // 4], in_=src[:, : Y_CAST_SPLIT // 4])
         combine(last, slice(HALF, N))
-        nc.vector.tensor_copy(out=dst[:, half:], in_=src[:, half:])
-        nc.vector.tensor_copy(out=dst[:, split:half], in_=src[:, split:half])
+        store_rows(slice(last, PACK), whole)
+        for first, end in ((HALF, N), (Y_CAST_SPLIT, HALF)):
+            nc.vector.tensor_copy(out=dst[:, first // 4 : end // 4], in_=src[:, first // 4 : end // 4])
         quantize(y_codes, y_plane, y_bf, HALF, HALF)
         nc.sync.dma_start(out=words_out[:, HALF:], in_=y_codes[:, HALF:])
         quantize(y_codes, y_plane, y_bf, 0, HALF)

@@ -21,9 +21,7 @@ PASS = P * PACK
 EPS = 0.01
 RIVAL_SHARE = 0.3
 SQUARE_SCALE = 1.0 / math.sqrt(N * EPS)
-HALF = N // 2
 X_LOADS = ((0, 0, 4), (1, 0, 2), (1, 2, 2))
-Y_CAST_SPLIT = 208
 
 
 def tile_mix_rows_sized_like_rival_pl_kernel(
@@ -85,7 +83,8 @@ def tile_mix_rows_sized_like_rival_pl_kernel(
             g, first, count = X_LOADS[i]
             src = x_raw[i][:].rearrange("p j (m r) -> p m j r", r=PACK)
             dst = x_bf[g][:].rearrange("p (r m j) -> p m j r", r=PACK, j=PACK)[:, :, first : first + count, :]
-            nc.vector.tensor_copy(out=dst[:, :, :, :2], in_=src[:, :, :, :2])
+            for tiles in ((slice(0, 1), slice(1, 2)) if i == len(X_LOADS) - 1 else (slice(0, 2),)):
+                nc.vector.tensor_copy(out=dst[:, :, :, tiles], in_=src[:, :, :, tiles])
             nc.scalar.copy(out=dst[:, :, :, 2:], in_=src[:, :, :, 2:])
 
         def quantize(codes, plane, values, first, count):
@@ -153,8 +152,8 @@ def tile_mix_rows_sized_like_rival_pl_kernel(
         load_x(2)
         load_plane(nc.sync, wa_plane, wa_scales)
         load_words(wc_codes[1], wc_words[1])
-        nc.sync.dma_start(out=wa_codes[:].bitcast(I32), in_=wa_words.bitcast(I32).rearrange("g p n -> p g n"))
         load_words(xs_raw, xs_words[0])
+        nc.sync.dma_start(out=wa_codes[:].bitcast(I32), in_=wa_words.bitcast(I32).rearrange("g p n -> p g n"))
         nc.sync.dma_start(out=ws_codes[:].bitcast(I32), in_=ws_words[0].bitcast(I32))
         load_plane(nc.sync, ws_plane, ws_scales)
 
@@ -171,23 +170,29 @@ def tile_mix_rows_sized_like_rival_pl_kernel(
         for r in range(PACK):
             nc.gpsimd.tensor_copy(out=xs_codes[:, r * P : (r + 1) * P], in_=xs_raw[:, r:T:PACK])
             nc.gpsimd.tensor_copy(out=xs_plane[:, r * P : (r + 1) * P], in_=xs_plane_raw[:, 0, r:T:PACK])
+
+        def wa_pass(r, g):
+            product(acc_a[r], x_codes[g], x_plane[g], r, wa_codes[:, g, :].bitcast(FP4X4), wa_plane[:, g, :], g == 0, False)
+
+        wa_pass(0, 0)
         for r in range(PACK):
-            for g in range(2):
-                product(acc_a[r], x_codes[g], x_plane[g], r, wa_codes[:, g, :].bitcast(FP4X4), wa_plane[:, g, :], g == 0, False)
+            wa_pass(r, 1)
+            if r + 1 < PACK:
+                wa_pass(r + 1, 0)
             product(acc_a[r], xs_codes, xs_plane, r, ws_codes[:].bitcast(FP4X4), ws_plane[:, 0, :], False, True)
 
         last = PACK - 1
         whole = slice(0, N)
-        take_b(0)
-        sum_squares(acc_b, sum_b, 1)
-        take_b(2)
         sum_squares(acc_b, sum_b, 0)
         take_b(1)
         sum_squares(acc_b, sum_b, 2)
-        take_b(last)
+        take_b(0)
+        sum_squares(acc_b, sum_b, 1)
+        take_b(2)
         add_one(slice(0, last))
-        sum_squares_on_vector(last)
+        take_b(last)
         invert(slice(0, last))
+        sum_squares_on_vector(last)
         add_one(slice(last, PACK))
         sum_squares(acc_a, sum_a, 0)
         sum_squares(acc_a, sum_a, 1)
@@ -206,16 +211,21 @@ def tile_mix_rows_sized_like_rival_pl_kernel(
         src = y[:].rearrange("p r (c i) -> p c r i", i=4)
         dst = y_bf[:].rearrange("p (c i r) -> p c r i", i=4, r=PACK)
         words_out = out_1[0].rearrange("p n t -> p (n t)").bitcast(I32)
-        combine(last, slice(0, HALF))
-        nc.scalar.copy(out=dst[:, : Y_CAST_SPLIT // 4], in_=src[:, : Y_CAST_SPLIT // 4])
-        combine(last, slice(HALF, N))
+
+        def cast_cols(first, end):
+            return dst[:, first // 4 : end // 4], src[:, first // 4 : end // 4]
+
+        combine(last, slice(0, P))
+        nc.scalar.copy(*cast_cols(0, P))
+        combine(last, slice(P, N))
+        nc.scalar.copy(*cast_cols(N - P, N))
         store_rows(slice(last, PACK), whole)
-        for first, end in ((HALF, N), (Y_CAST_SPLIT, HALF)):
-            nc.vector.tensor_copy(out=dst[:, first // 4 : end // 4], in_=src[:, first // 4 : end // 4])
-        quantize(y_codes, y_plane, y_bf, HALF, HALF)
-        nc.sync.dma_start(out=words_out[:, HALF:], in_=y_codes[:, HALF:])
-        quantize(y_codes, y_plane, y_bf, 0, HALF)
-        nc.sync.dma_start(out=words_out[:, :HALF], in_=y_codes[:, :HALF])
+        nc.vector.tensor_copy(*cast_cols(P, N - P))
+        quantize(y_codes, y_plane, y_bf, 0, P)
+        quantize(y_codes, y_plane, y_bf, P, N - 2 * P)
+        nc.sync.dma_start(out=words_out[:, : N - P], in_=y_codes[:, : N - P])
+        quantize(y_codes, y_plane, y_bf, N - P, P)
+        nc.sync.dma_start(out=words_out[:, N - P :], in_=y_codes[:, N - P :])
         for q in range(4):
             queue = nc.scalar if q % 2 == 0 else nc.sync
             queue.dma_start(out=out_2[0].bitcast(I32)[4 * q : 4 * q + 4, :], in_=y_plane[:].bitcast(I32)[32 * q : 32 * q + 4, :])

import math
from contextlib import ExitStack

import concourse.mybir as mybir

K, L, T, N = 1024, 512, 512, 512
FLOPS = 2 * T * N * (K + L + K)

F32 = mybir.dt.float32
BF16 = mybir.dt.bfloat16
I32 = mybir.dt.int32
U8 = mybir.dt.uint8
FP8X4 = mybir.dt.float8_e4m3fn_x4
FP4X4 = mybir.dt.float4_e2m1fn_x4
ACT = mybir.ActivationFunctionType
ALU = mybir.AluOpType

P = 128
PACK = 4
PASS = P * PACK
EPS = 0.01
RIVAL_SHARE = 0.3
SQUARE_SCALE = 1.0 / math.sqrt(N * EPS)
X_LOADS = ((0, 0, 4), (1, 0, 2), (1, 2, 2))


def tile_mix_rows_sized_like_rival_pl_kernel(
    tc, xt, wa_words, wa_scales, xs_words, xs_scales, ws_words, ws_scales, wc_words, wc_scales, out_0, out_1, out_2
):
    nc = tc.nc
    with ExitStack() as ctx:
        sb = ctx.enter_context(tc.tile_pool(name="sb", bufs=1))
        ps = ctx.enter_context(tc.psum_pool(name="ps", bufs=1))
        ctx.enter_context(tc.manual_schedule())

        x_raw = [sb.tile([P, count, T], F32, name="x_raw%d" % i) for i, (g, first, count) in enumerate(X_LOADS)]
        x_bf = [sb.tile([P, T * PACK], BF16, name="x_bf%d" % g, align_bytes=64) for g in range(2)]
        x_codes = [sb.tile([P, T], I32, name="x_codes%d" % g, align_bytes=64) for g in range(2)]
        x_plane = [sb.tile([P, T], U8, name="x_plane%d" % g, align_bytes=64) for g in range(2)]
        wc_codes = [sb.tile([P, N], I32, name="wc_codes%d" % g, align_bytes=64) for g in range(2)]
        wc_plane = sb.tile([P, 2, N], U8, align_bytes=64)
        wa_codes = sb.tile([P, 2, 2 * N], U8, align_bytes=64)
        wa_plane = sb.tile([P, 2, N], U8, align_bytes=64)
        ws_codes = sb.tile([P, 2 * N], U8, align_bytes=64)
        ws_plane = sb.tile([P, 1, N], U8, align_bytes=64)
        xs_raw = sb.tile([P, T], I32, align_bytes=64)
        xs_plane_raw = sb.tile([P, 1, T], U8, align_bytes=64)
        xs_codes = sb.tile([P, T], I32, align_bytes=64)
        xs_plane = sb.tile([P, T], U8, align_bytes=64)
        b_part = [sb.tile([P, N], F32, name="b_part%d" % r) for r in range(PACK)]
        y = sb.tile([P, PACK, N], F32)
        y_bf = sb.tile([P, N * PACK], BF16, align_bytes=64)
        y_codes = sb.tile([P, N], I32, align_bytes=64)
        y_plane = sb.tile([P, N], U8, align_bytes=64)
        sum_b = sb.tile([P, PACK], F32)
        sum_b1 = sb.tile([P, PACK], F32)
        inv_b = sb.tile([P, PACK], F32)
        sum_a = sb.tile([P, PACK], F32)
        gain = sb.tile([P, PACK], F32)
        table = sb.tile([P, 1], F32)
        acc_a = [ps.tile([P, N], F32, name="acc_a%d" % r) for r in range(PACK)]
        acc_b = [ps.tile([P, N], F32, name="acc_b%d" % r) for r in range(PACK)]

        def zero(engine, plane):
            engine.memset(plane[:].rearrange("p g n -> p (g n)").bitcast(I32), 0)

        def load_plane(queue, plane, scales):
            for r in range(4):
                queue.dma_start(
                    out=plane[:].bitcast(I32)[r:P:32],
                    in_=scales.bitcast(I32)[:, r:16:4, :].rearrange("g q n -> q g n"),
                )

        def load_x(i):
            g, first, count = X_LOADS[i]
            rows = xt[g * PASS : (g + 1) * PASS, :].rearrange("(p j) t -> p j t", j=PACK)
            nc.sync.dma_start(out=x_raw[i][:], in_=rows[:, first : first + count, :])

        def load_words(tile, words):
            nc.sync.dma_start(out=tile[:], in_=words.rearrange("p n t -> p (n t)").bitcast(I32))

        def cast_x(i):
            g, first, count = X_LOADS[i]
            src = x_raw[i][:].rearrange("p j (m r) -> p m j r", r=PACK)
            dst = x_bf[g][:].rearrange("p (r m j) -> p m j r", r=PACK, j=PACK)[:, :, first : first + count, :]
            for tiles in ((slice(0, 1), slice(1, 2)) if i == len(X_LOADS) - 1 else (slice(0, 2),)):
                nc.vector.tensor_copy(out=dst[:, :, :, tiles], in_=src[:, :, :, tiles])
            nc.scalar.copy(out=dst[:, :, :, 2:], in_=src[:, :, :, 2:])

        def quantize(codes, plane, values, first, count):
            nc.vector.quantize_mx(
                out=codes[:, first : first + count].bitcast(FP8X4),
                scales=plane[:, first : first + count],
                in_=values[:, PACK * first : PACK * (first + count)],
            )

        def product(acc, codes, plane, r, w, w_plane, start, stop):
            cols = slice(r * P, (r + 1) * P)
            nc.tensor.matmul_mx(
                out=acc[:], lhsT=codes[:, cols].bitcast(FP8X4), lhsT_scale=plane[:, cols],
                rhs=w, rhs_scale=w_plane, start=start, stop=stop,
            )

        def sum_squares(acc, sums, r):
            nc.scalar.activation(
                out=y[:, r, :], in_=acc[r][:], func=ACT.Square, scale=SQUARE_SCALE, accum_out=sums[:, r : r + 1]
            )

        def row_gain(r):
            col = slice(r, r + 1)
            nc.scalar.activation(
                out=gain[:, col], in_=sum_a[:, col], func=ACT.Abs_reciprocal_sqrt, scale=inv_b[:, col], bias=inv_b[:, col]
            )

        def take_b(r):
            nc.vector.tensor_scalar(out=b_part[r][:], in0=acc_b[r][:], scalar1=RIVAL_SHARE, scalar2=None, op0=ALU.mult)

        def sum_squares_on_vector(r):
            nc.vector.scalar_tensor_tensor(
                out=y[:, r, :], in0=acc_b[r][:], scalar=1.0 / (RIVAL_SHARE * N * EPS), in1=b_part[r][:],
                op0=ALU.mult, op1=ALU.mult, accum_out=sum_b[:, r : r + 1],
            )

        def add_one(cols):
            nc.vector.tensor_scalar(out=sum_b1[:, cols], in0=sum_b[:, cols], scalar1=1.0, scalar2=None, op0=ALU.add)

        def invert(cols):
            nc.vector.reciprocal(out=inv_b[:, cols], in_=sum_b1[:, cols])

        out_rows = out_0.rearrange("(p r) n -> p r n", r=PACK)

        def combine(r, cols):
            nc.vector.scalar_tensor_tensor(
                out=y[:, r, cols], in0=acc_a[r][:, cols], scalar=gain[:, r : r + 1], in1=b_part[r][:, cols],
                op0=ALU.mult, op1=ALU.add,
            )

        def store_rows(rows, cols):
            nc.sync.dma_start(out=out_rows[:, rows, cols], in_=y[:, rows, cols])

        zero(nc.vector, wc_plane)
        zero(nc.vector, wa_plane)
        zero(nc.vector, ws_plane)
        nc.vector.memset(table[:], 1.0)
        nc.scalar.activation(out=gain[:, 0:1], in_=table[:], func=ACT.Abs_reciprocal_sqrt)
        zero(nc.gpsimd, xs_plane_raw)
        load_plane(nc.gpsimd, xs_plane_raw, xs_scales)
        load_x(0)
        load_plane(nc.sync, wc_plane, wc_scales)
        load_words(wc_codes[0], wc_words[0])
        load_x(1)
        load_x(2)
        load_plane(nc.sync, wa_plane, wa_scales)
        load_words(wc_codes[1], wc_words[1])
        load_words(xs_raw, xs_words[0])
        nc.sync.dma_start(out=wa_codes[:].bitcast(I32), in_=wa_words.bitcast(I32).rearrange("g p n -> p g n"))
        nc.sync.dma_start(out=ws_codes[:].bitcast(I32), in_=ws_words[0].bitcast(I32))
        load_plane(nc.sync, ws_plane, ws_scales)

        cast_x(0)
        for r in range(PACK):
            quantize(x_codes[0], x_plane[0], x_bf[0], r * P, P)
            product(acc_b[r], x_codes[0], x_plane[0], r, wc_codes[0][:].bitcast(FP8X4), wc_plane[:, 0, :], True, False)

        cast_x(1)
        cast_x(2)
        for r in range(PACK):
            quantize(x_codes[1], x_plane[1], x_bf[1], r * P, P)
            product(acc_b[r], x_codes[1], x_plane[1], r, wc_codes[1][:].bitcast(FP8X4), wc_plane[:, 1, :], False, True)
        for r in range(PACK):
            nc.gpsimd.tensor_copy(out=xs_codes[:, r * P : (r + 1) * P], in_=xs_raw[:, r:T:PACK])
            nc.gpsimd.tensor_copy(out=xs_plane[:, r * P : (r + 1) * P], in_=xs_plane_raw[:, 0, r:T:PACK])

        def wa_pass(r, g):
            product(acc_a[r], x_codes[g], x_plane[g], r, wa_codes[:, g, :].bitcast(FP4X4), wa_plane[:, g, :], g == 0, False)

        wa_pass(0, 0)
        for r in range(PACK):
            wa_pass(r, 1)
            if r + 1 < PACK:
                wa_pass(r + 1, 0)
            product(acc_a[r], xs_codes, xs_plane, r, ws_codes[:].bitcast(FP4X4), ws_plane[:, 0, :], False, True)

        last = PACK - 1
        whole = slice(0, N)
        sum_squares(acc_b, sum_b, 0)
        take_b(1)
        sum_squares(acc_b, sum_b, 2)
        take_b(0)
        sum_squares(acc_b, sum_b, 1)
        take_b(2)
        add_one(slice(0, last))
        take_b(last)
        invert(slice(0, last))
        sum_squares_on_vector(last)
        add_one(slice(last, PACK))
        sum_squares(acc_a, sum_a, 0)
        sum_squares(acc_a, sum_a, 1)
        row_gain(0)
        combine(0, whole)
        store_rows(slice(0, 1), whole)
        invert(slice(last, PACK))
        for r in range(1, PACK):
            if r > 1:
                sum_squares(acc_a, sum_a, r)
            row_gain(r)
            if r < last:
                combine(r, whole)
                store_rows(slice(r, r + 1), whole)

        src = y[:].rearrange("p r (c i) -> p c r i", i=4)
        dst = y_bf[:].rearrange("p (c i r) -> p c r i", i=4, r=PACK)
        words_out = out_1[0].rearrange("p n t -> p (n t)").bitcast(I32)

        def cast_cols(first, end):
            return dst[:, first // 4 : end // 4], src[:, first // 4 : end // 4]

        combine(last, slice(0, P))
        nc.scalar.copy(*cast_cols(0, P))
        combine(last, slice(P, N))
        nc.scalar.copy(*cast_cols(N - P, N))
        store_rows(slice(last, PACK), whole)
        nc.vector.tensor_copy(*cast_cols(P, N - P))
        quantize(y_codes, y_plane, y_bf, 0, P)
        quantize(y_codes, y_plane, y_bf, P, N - 2 * P)
        nc.sync.dma_start(out=words_out[:, : N - P], in_=y_codes[:, : N - P])
        quantize(y_codes, y_plane, y_bf, N - P, P)
        nc.sync.dma_start(out=words_out[:, N - P :], in_=y_codes[:, N - P :])
        for q in range(4):
            queue = nc.scalar if q % 2 == 0 else nc.sync
            queue.dma_start(out=out_2[0].bitcast(I32)[4 * q : 4 * q + 4, :], in_=y_plane[:].bitcast(I32)[32 * q : 32 * q + 4, :])
